import numpy as np
import ml_dtypes


def mxq(x, axis, fmt="e4m3"):
    dtype, down = {"e4m3": (ml_dtypes.float8_e4m3fn, 7), "e5m2": (ml_dtypes.float8_e5m2, 14)}[fmt]
    v = np.moveaxis(np.asarray(x, np.float32).astype(ml_dtypes.bfloat16).astype(np.float64), axis, -1)
    blocks = v.reshape(v.shape[:-1] + (-1, 32))
    amax = np.abs(blocks).max(-1, keepdims=True)
    byte = np.maximum(np.where(amax > 0, np.frexp(amax)[1] - 1 + 127, 0) - down, 1)
    scale = np.exp2(byte - 127.0)
    codes = (blocks / scale).astype(np.float32).astype(dtype).astype(np.float64)
    return np.moveaxis((codes * scale).reshape(v.shape), -1, axis)


WIDE = False


def mx_kscale(k):
    if not WIDE:
        return np.ones(k)
    levels = np.array([10, -10, 5, -5, 0])
    if k % 512:
        return np.exp2(np.random.permutation(np.resize(levels, k // 32))).repeat(32)
    a = np.empty((k // 512, 16))
    for p in range(k // 512):
        a[p, :8] = np.random.permutation(np.resize(levels, 8))
        for g in range(8):
            far = levels[np.abs(levels - a[p, g]) >= 10]
            a[p, g + 8] = far[np.random.randint(len(far))]
    return np.exp2(a.ravel()).repeat(32)


def f64(x):
    return np.asarray(x).astype(np.float64)


def striped(idx):
    return np.tile(idx.reshape(-1, 16).T, (8, 1)).astype(np.uint16)


def unstriped(offs):
    return offs[:16].T.reshape(-1).astype(np.int64)


def striped8(idx):
    return np.concatenate([x.reshape(-1, 16).T for x in idx]).astype(np.uint16)


def runs(offs, k):
    lists = np.stack([offs[16 * r : 16 * r + 16].T.reshape(-1) for r in range(8)]).astype(np.int64)
    return lists[np.arange(k) % 512 // 64]


def pack_weight(w):
    k, n = w.shape
    w = f64(np.asarray(w, np.float32).astype(ml_dtypes.bfloat16)).reshape(k // 32, 32, n)
    amax = np.abs(w).max(1)
    byte = np.clip(np.where(amax > 0, np.frexp(amax)[1] - 1 + 127 - 7, 1), 1, 254)
    scaled = (w * np.exp2(127.0 - byte)[:, None, :]).reshape(k, n).astype(np.float32)
    words = np.ascontiguousarray(scaled.reshape(k // 512, 128, 4, n).transpose(0, 1, 3, 2)).astype(ml_dtypes.float8_e4m3fn).view(np.uint8)
    return words, np.ascontiguousarray(byte.astype(np.uint8).reshape(k // 512, 16, n))


def unpack_weight(words, scales):
    g, p, n, _ = words.shape
    vals = np.ascontiguousarray(words).view(ml_dtypes.float8_e4m3fn).astype(np.float64) * np.repeat(np.exp2(scales.astype(np.float64) - 127.0), 8, axis=1)[..., None]
    return vals.transpose(0, 1, 3, 2).reshape(g * 512, n)

def planes(y):
    n, m = y.shape
    v = y.astype(np.float32).astype(ml_dtypes.bfloat16).astype(np.float64).reshape(n // 32, 32, m)
    top = np.abs(v).max(1)
    byte = np.clip(np.where(top > 0, np.frexp(top)[1] - 1 + 127 - 7, 1), 1, 254)
    codes = (v * np.exp2(127.0 - byte)[:, None, :]).reshape(n, m).astype(np.float32).astype(ml_dtypes.float8_e4m3fn).view(np.uint8)
    words = codes.reshape(n // 512, 128, 4, m).transpose(0, 1, 3, 2)
    return np.ascontiguousarray(words), np.ascontiguousarray(byte.astype(np.uint8).reshape(n // 512, 16, m))


K, T, S, N, W = 512, 2048, 512, 512, 256


def setup_inputs():
    n = np.random.standard_normal
    s = mx_kscale(K)[:, None]
    packed_xT = pack_weight(n((K, T)) * s)
    perm = np.stack([np.random.permutation(S) for _ in range(8)])
    return {
        "x_words": packed_xT[0],
        "x_scales": packed_xT[1],
        "w1": (n((K, N)) / np.sqrt(2 * K) / s).astype(np.float32),
        "w2": (n((K, N)) / np.sqrt(2 * K) / s).astype(np.float32),
        "offs": striped(np.random.permutation(T)[:S]),
        "hz": striped8(np.random.randint(0, T, (8, S))),
        "n1": striped8(perm[:, :W]),
        "n2": striped8(perm[:, W:]),
    }


def reference(x_words, x_scales, w1, w2, offs, hz, n1, n2):
    xq = unpack_weight(x_words, x_scales)[:, unstriped(offs)]
    x_hz = unpack_weight(x_words, x_scales)[np.arange(K)[:, None], runs(hz, K)]
    h = mxq(f64(w1), 0, "e4m3").T @ xq + mxq(f64(w2), 0, "e4m3").T @ x_hz
    pa = h[np.arange(N)[:, None], runs(n1, N)]
    pb = h[np.arange(N)[:, None], runs(n2, N)]
    rb = np.maximum(pa, pb)
    ra = pa / (np.abs(pb) + 0.5)
    ds = np.zeros((N, S))
    ds[np.arange(N)[:, None], runs(n1, N)] = ra
    out = ds.copy()
    out[np.arange(N)[:, None], runs(n2, N)] = rb
    return (out,) + planes(out)

@@ -1,0 +1,142 @@
+from contextlib import ExitStack
+
+import concourse.mybir as mybir
+
+F32 = mybir.dt.float32
+BF16 = mybir.dt.bfloat16
+I32 = mybir.dt.int32
+U32 = mybir.dt.uint32
+U16 = mybir.dt.uint16
+U8 = mybir.dt.uint8
+FP8X4 = mybir.dt.float8_e4m3fn_x4
+ACT = mybir.ActivationFunctionType
+ALU = mybir.AluOpType
+
+P = 128
+PACK = 4
+K, T, S, N, W = 512, 2048, 512, 512, 256
+HALF = N // 2
+FLOPS = 2 * 2 * K * N * S
+
+
+def tile_picked_othratio_none_po_kernel(tc, x_words, x_scales, w1, w2, offs, hz, n1, n2, out_0, out_1, out_2):
+    nc = tc.nc
+    with ExitStack() as ctx:
+        keep = ctx.enter_context(tc.tile_pool(name="keep", bufs=1))
+        psum = ctx.enter_context(tc.psum_pool(name="psum", bufs=1))
+
+        offs_sb = keep.tile([P, S // 16], U16, name="offs_sb")
+        hz_sb = keep.tile([P, S // 16], U16, name="hz_sb")
+        n1_sb = keep.tile([P, W // 16], U16, name="n1_sb")
+        n2_sb = keep.tile([P, W // 16], U16, name="n2_sb")
+        table_words = keep.tile([P, T], U32, name="table_words", align_bytes=64)
+        table_scales = keep.tile([P, T], U8, name="table_scales", align_bytes=64)
+        picked_scales = keep.tile([P, 2 * S], U8, name="picked_scales", align_bytes=64)
+        x_planes = keep.tile([P, 2 * S], U8, name="x_planes", align_bytes=64)
+        half = keep.tile([P, 1], F32, name="half")
+
+        nc.gpsimd.memset(table_scales[:].bitcast(I32), 0)
+        nc.scalar.dma_start(out=table_scales[0:P:8, :].bitcast(I32), in_=x_scales[0].bitcast(I32))
+        nc.sync.dma_start(hz_sb[:], hz)
+        nc.sync.dma_start(offs_sb[:], offs)
+        nc.sync.dma_start(out=table_words[:].bitcast(I32), in_=x_words[0].rearrange("p c r -> p (c r)").bitcast(I32))
+        nc.sync.dma_start(n2_sb[:], n2)
+        nc.sync.dma_start(n1_sb[:], n1)
+        raw = {}
+        for i, w in enumerate((w1, w2)):
+            for c in range(2):
+                raw[i, c] = keep.tile([P, PACK, HALF], F32, name=f"raw{i}{c}", align_bytes=64)
+                nc.sync.dma_start(out=raw[i, c][:], in_=w[:, c * HALF:(c + 1) * HALF].rearrange("(p j) c -> p j c", j=PACK))
+        nc.gpsimd.memset(x_planes[:].bitcast(I32), 0)
+        nc.gpsimd.memset(half[:], 0.5)
+
+        nc.vector.tensor_copy(picked_scales[:, S:], table_scales[:].indirect(hz_sb[:]))
+        nc.vector.tensor_copy(picked_scales[:, :S], table_scales[:].indirect(offs_sb[:]))
+        for j in range(PACK):
+            nc.scalar.dma_start(out=x_planes[j:P:32, :].bitcast(I32), in_=picked_scales[8 * j:P:32, :].bitcast(I32))
+        picked_words = []
+        for i, lst in enumerate((offs_sb, hz_sb)):
+            words = keep.tile([P, S], U32, name=f"picked_words{i}", align_bytes=64)
+            nc.vector.tensor_copy(words[:], table_words[:].indirect(lst[:]))
+            picked_words.append(words)
+
+        dealt = [keep.tile([P, PACK, P, PACK], BF16, name=f"dealt{i}", align_bytes=64) for i in range(2)]
+        w_codes = [keep.tile([P, N], U32, name=f"w_codes{i}", align_bytes=64) for i in range(2)]
+        w_planes = [keep.tile([P, N], U8, name=f"w_planes{i}", align_bytes=64) for i in range(2)]
+
+        def deal(copy, i, c, m0, m1):
+            base = c * (HALF // PACK)
+            copy(out=dealt[i][:, :, base + m0:base + m1, :].rearrange("p t m j -> p m j t"),
+                 in_=raw[i, c][:, :, PACK * m0:PACK * m1].rearrange("p j (m t) -> p m j t", t=PACK))
+
+        def quantize_weights(i, t0, t1):
+            nc.vector.quantize_mx(out=w_codes[i][:, t0 * P:t1 * P].bitcast(FP8X4), scales=w_planes[i][:, t0 * P:t1 * P],
+                                  in_=dealt[i][:, t0:t1].rearrange("p t m j -> p (t m j)"))
+
+        deal(nc.scalar.copy, 0, 0, 0, 64)
+        deal(nc.scalar.copy, 0, 1, 0, 64)
+        deal(nc.vector.tensor_copy, 1, 0, 0, 64)
+        quantize_weights(0, 0, PACK)
+        deal(nc.vector.tensor_copy, 1, 1, 0, 44)
+        deal(nc.scalar.copy, 1, 1, 44, 64)
+        for t in range(PACK):
+            quantize_weights(1, t, t + 1)
+
+        banks = [(0, slice(0, S // 2)), (0, slice(S // 2, S))] + [(t, slice(0, S)) for t in range(1, PACK)]
+        acc = [psum.tile([P, cols.stop - cols.start], F32, name=f"acc{b}") for b, (t, cols) in enumerate(banks)]
+        for b, (t, cols) in enumerate(banks):
+            for i in range(2):
+                rows = slice(t * P, (t + 1) * P)
+                nc.tensor.matmul_mx(out=acc[b][:], lhsT=w_codes[i][:, rows].bitcast(FP8X4), lhsT_scale=w_planes[i][:, rows],
+                                    rhs=picked_words[i][:, cols].bitcast(FP8X4),
+                                    rhs_scale=x_planes[:, i * S + cols.start:i * S + cols.stop],
+                                    start=(i == 0), stop=(i == 1))
+
+        def tiles(name, width):
+            return [keep.tile([P, width], F32, name=f"{name}{t}", align_bytes=64) for t in range(PACK)]
+
+        h, y = [keep.tile([P, S], F32, name="h", align_bytes=64)] * PACK, tiles("y", S)
+        pa, pb, rb, size, root, inv = (tiles(name, W) for name in ("pa", "pb", "rb", "size", "root", "inv"))
+        rounded = keep.tile([P, PACK, S], BF16, name="rounded", align_bytes=64)
+        out_rows = out_0.rearrange("(p t) c -> t p c", t=PACK)
+
+        nc.vector.tensor_copy(out=h[0][:, :S // 2], in_=acc[0][:])
+        nc.scalar.copy(out=h[0][:, S // 2:], in_=acc[1][:])
+        nc.scalar.activation(pb[0][:], h[0][:].indirect(n2_sb[:]), ACT.Copy)
+        nc.vector.tensor_copy(pa[0][:], h[0][:].indirect(n1_sb[:]))
+        nc.vector.tensor_tensor(rb[0][:], pa[0][:], pb[0][:], ALU.max)
+        for t in range(PACK):
+            u = t + 1
+            nc.vector.tensor_copy(y[t][:].indirect(n2_sb[:]), rb[t][:])
+            if u < PACK:
+                nc.scalar.copy(out=h[u][:], in_=acc[u + 1][:])
+            nc.scalar.activation(size[t][:], pb[t][:], ACT.Abs)
+            if u < PACK:
+                nc.scalar.activation(pb[u][:], h[u][:].indirect(n2_sb[:]), ACT.Copy)
+            nc.scalar.activation(root[t][:], size[t][:], ACT.Abs_reciprocal_sqrt, bias=half[:])
+            if u < PACK:
+                nc.scalar.activation(pa[u][:], h[u][:].indirect(n1_sb[:]), ACT.Copy)
+            nc.scalar.activation(inv[t][:], root[t][:], ACT.Square)
+            if u < PACK:
+                nc.vector.tensor_tensor(rb[u][:], pa[u][:], pb[u][:], ALU.max)
+            nc.vector.tensor_tensor(y[t][:].indirect(n1_sb[:]), pa[t][:], inv[t][:], ALU.mult)
+            nc.sync.dma_start(out=out_rows[t], in_=y[t][:])
+        for t in range(PACK - 1):
+            nc.scalar.copy(out=rounded[:, t, :], in_=y[t][:])
+        nc.vector.tensor_copy(out=rounded[:, PACK - 1, :], in_=y[PACK - 1][:])
+
+        woven = keep.tile([P, S, PACK], BF16, name="woven", align_bytes=64)
+        y_codes = keep.tile([P, S], U32, name="y_codes", align_bytes=64)
+        y_plane = keep.tile([P, S], U8, name="y_plane", align_bytes=64)
+        out_words = out_1[0].rearrange("p c r -> p (c r)").bitcast(I32)
+        for copy, cols in ((nc.vector.tensor_copy, slice(0, 256)), (nc.vector.tensor_copy, slice(256, 320)), (nc.scalar.copy, slice(320, S))):
+            copy(out=woven[:, cols, :].rearrange("p (c i) t -> p c t i", i=4),
+                 in_=rounded[:, :, cols].rearrange("p t (c i) -> p c t i", i=4))
+        for c in range(2):
+            cols = slice(c * S // 2, (c + 1) * S // 2)
+            nc.vector.quantize_mx(out=y_codes[:, cols].bitcast(FP8X4), scales=y_plane[:, cols],
+                                  in_=woven[:, cols, :].rearrange("p c t -> p (c t)"))
+            nc.sync.dma_start(out=out_words[:, cols], in_=y_codes[:, cols].bitcast(I32))
+        for q in range(4):
+            queue = nc.sync if q % 2 == 0 else nc.scalar
+            queue.dma_start(out=out_2[0, 4 * q:4 * q + 4, :].bitcast(I32), in_=y_plane[32 * q:32 * q + 4, :].bitcast(I32))

@@ -49,6 +49,8 @@ def tile_picked_othratio_none_po_kernel(tc, x_words, x_scales, w1, w2, offs, hz,
                 nc.sync.dma_start(out=raw[i, c][:], in_=w[:, c * HALF:(c + 1) * HALF].rearrange("(p j) c -> p j c", j=PACK))
         nc.gpsimd.memset(x_planes[:].bitcast(I32), 0)
         nc.gpsimd.memset(half[:], 0.5)
+        warm = keep.tile([P, 1], F32, name="warm")
+        nc.scalar.activation(warm[:], half[:], ACT.Abs_reciprocal_sqrt)
 
         nc.vector.tensor_copy(picked_scales[:, S:], table_scales[:].indirect(hz_sb[:]))
         nc.vector.tensor_copy(picked_scales[:, :S], table_scales[:].indirect(offs_sb[:]))

@@ -35,20 +35,22 @@ def tile_picked_othratio_none_po_kernel(tc, x_words, x_scales, w1, w2, offs, hz,
         x_planes = keep.tile([P, 2 * S], U8, name="x_planes", align_bytes=64)
         half = keep.tile([P, 1], F32, name="half")
 
-        nc.gpsimd.memset(table_scales[:].bitcast(I32), 0)
-        nc.scalar.dma_start(out=table_scales[0:P:8, :].bitcast(I32), in_=x_scales[0].bitcast(I32))
+        nc.sync.dma_start(out=table_scales[:].bitcast(I32),
+                          in_=x_scales[0].bitcast(I32).unsqueeze(1).to_broadcast([16, 8, T // 4]))
         nc.sync.dma_start(hz_sb[:], hz)
         nc.sync.dma_start(offs_sb[:], offs)
         nc.sync.dma_start(out=table_words[:].bitcast(I32), in_=x_words[0].rearrange("p c r -> p (c r)").bitcast(I32))
         nc.sync.dma_start(n2_sb[:], n2)
         nc.sync.dma_start(n1_sb[:], n1)
-        raw = {}
-        for i, w in enumerate((w1, w2)):
-            for c in range(2):
-                raw[i, c] = keep.tile([P, PACK, HALF], F32, name=f"raw{i}{c}", align_bytes=64)
-                nc.sync.dma_start(out=raw[i, c][:], in_=w[:, c * HALF:(c + 1) * HALF].rearrange("(p j) c -> p j c", j=PACK))
-        nc.gpsimd.memset(x_planes[:].bitcast(I32), 0)
+        raw1 = keep.tile([P, PACK, N], F32, name="raw1", align_bytes=64)
+        nc.sync.dma_start(out=raw1[:], in_=w1.rearrange("(p j) c -> p j c", j=PACK))
+        raw = {(0, c): raw1[:, :, c * HALF:(c + 1) * HALF] for c in range(2)}
+        for c in range(2):
+            raw2 = keep.tile([P, PACK, HALF], F32, name=f"raw2{c}", align_bytes=64)
+            nc.sync.dma_start(out=raw2[:], in_=w2[:, c * HALF:(c + 1) * HALF].rearrange("(p j) c -> p j c", j=PACK))
+            raw[1, c] = raw2[:]
         nc.gpsimd.memset(half[:], 0.5)
+        nc.gpsimd.memset(x_planes[:].bitcast(I32), 0)
         warm = keep.tile([P, 1], F32, name="warm")
         nc.scalar.activation(warm[:], half[:], ACT.Abs_reciprocal_sqrt)
 
@@ -62,34 +64,36 @@ def tile_picked_othratio_none_po_kernel(tc, x_words, x_scales, w1, w2, offs, hz,
             nc.vector.tensor_copy(words[:], table_words[:].indirect(lst[:]))
             picked_words.append(words)
 
-        dealt = [keep.tile([P, PACK, P, PACK], BF16, name=f"dealt{i}", align_bytes=64) for i in range(2)]
-        w_codes = [keep.tile([P, N], U32, name=f"w_codes{i}", align_bytes=64) for i in range(2)]
-        w_planes = [keep.tile([P, N], U8, name=f"w_planes{i}", align_bytes=64) for i in range(2)]
+        dealt = keep.tile([P, PACK, 2, P, PACK], BF16, name="dealt", align_bytes=64)
+        w_codes = keep.tile([P, 2 * N], U32, name="w_codes", align_bytes=64)
+        w_planes = keep.tile([P, 2 * N], U8, name="w_planes", align_bytes=64)
 
         def deal(copy, i, c, m0, m1):
             base = c * (HALF // PACK)
-            copy(out=dealt[i][:, :, base + m0:base + m1, :].rearrange("p t m j -> p m j t"),
+            copy(out=dealt[:, :, i, base + m0:base + m1, :].rearrange("p t m j -> p m j t"),
                  in_=raw[i, c][:, :, PACK * m0:PACK * m1].rearrange("p j (m t) -> p m j t", t=PACK))
 
-        def quantize_weights(i, t0, t1):
-            nc.vector.quantize_mx(out=w_codes[i][:, t0 * P:t1 * P].bitcast(FP8X4), scales=w_planes[i][:, t0 * P:t1 * P],
-                                  in_=dealt[i][:, t0:t1].rearrange("p t m j -> p (t m j)"))
+        def quantize_weights(s0, s1):
+            nc.vector.quantize_mx(out=w_codes[:, s0 * P:s1 * P].bitcast(FP8X4), scales=w_planes[:, s0 * P:s1 * P],
+                                  in_=dealt[:].rearrange("p t i m j -> p (t i m j)")[:, s0 * N:s1 * N])
 
-        deal(nc.scalar.copy, 0, 0, 0, 64)
-        deal(nc.scalar.copy, 0, 1, 0, 64)
-        deal(nc.vector.tensor_copy, 1, 0, 0, 64)
-        quantize_weights(0, 0, PACK)
-        deal(nc.vector.tensor_copy, 1, 1, 0, 44)
-        deal(nc.scalar.copy, 1, 1, 44, 64)
-        for t in range(PACK):
-            quantize_weights(1, t, t + 1)
+        deal(nc.scalar.copy, 0, 0, 0, 40)
+        deal(nc.vector.tensor_copy, 0, 0, 40, 64)
+        deal(nc.vector.tensor_copy, 0, 1, 0, 64)
+        quantize_weights(0, 1)
+        for c in range(2):
+            deal(nc.vector.tensor_copy, 1, c, 0, 44)
+            deal(nc.scalar.copy, 1, c, 44, 64)
+        quantize_weights(1, 2)
+        for t in range(1, PACK):
+            quantize_weights(2 * t, 2 * t + 2)
 
         banks = [(0, slice(0, S // 2)), (0, slice(S // 2, S))] + [(t, slice(0, S)) for t in range(1, PACK)]
         acc = [psum.tile([P, cols.stop - cols.start], F32, name=f"acc{b}") for b, (t, cols) in enumerate(banks)]
         for b, (t, cols) in enumerate(banks):
             for i in range(2):
-                rows = slice(t * P, (t + 1) * P)
-                nc.tensor.matmul_mx(out=acc[b][:], lhsT=w_codes[i][:, rows].bitcast(FP8X4), lhsT_scale=w_planes[i][:, rows],
+                rows = slice((2 * t + i) * P, (2 * t + i + 1) * P)
+                nc.tensor.matmul_mx(out=acc[b][:], lhsT=w_codes[:, rows].bitcast(FP8X4), lhsT_scale=w_planes[:, rows],
                                     rhs=picked_words[i][:, cols].bitcast(FP8X4),
                                     rhs_scale=x_planes[:, i * S + cols.start:i * S + cols.stop],
                                     start=(i == 0), stop=(i == 1))
@@ -97,9 +101,10 @@ def tile_picked_othratio_none_po_kernel(tc, x_words, x_scales, w1, w2, offs, hz,
         def tiles(name, width):
             return [keep.tile([P, width], F32, name=f"{name}{t}", align_bytes=64) for t in range(PACK)]
 
-        h, y = [keep.tile([P, S], F32, name="h", align_bytes=64)] * PACK, tiles("y", S)
-        pa, pb, rb, size, root, inv = (tiles(name, W) for name in ("pa", "pb", "rb", "size", "root", "inv"))
-        rounded = keep.tile([P, PACK, S], BF16, name="rounded", align_bytes=64)
+        h = [keep.tile([P, S], F32, name="h", tag="row", align_bytes=64)] * PACK
+        y = [keep.tile([P, S], F32, name=f"y{t}", tag=("row" if t == 2 else f"y{t}"), align_bytes=64) for t in range(PACK)]
+        pa, pb, rb, size, inv = (tiles(name, W) for name in ("pa", "pb", "rb", "size", "inv"))
+        root = [keep.tile([P, W], F32, name=f"root{t}", tag=("late" if t == PACK - 1 else f"root{t}"), align_bytes=64) for t in range(PACK)]
         out_rows = out_0.rearrange("(p t) c -> t p c", t=PACK)
 
         nc.vector.tensor_copy(out=h[0][:, :S // 2], in_=acc[0][:])
@@ -107,9 +112,17 @@ def tile_picked_othratio_none_po_kernel(tc, x_words, x_scales, w1, w2, offs, hz,
         nc.scalar.activation(pb[0][:], h[0][:].indirect(n2_sb[:]), ACT.Copy)
         nc.vector.tensor_copy(pa[0][:], h[0][:].indirect(n1_sb[:]))
         nc.vector.tensor_tensor(rb[0][:], pa[0][:], pb[0][:], ALU.max)
+        def put_max(t):
+            nc.vector.tensor_copy(y[t][:].indirect(n2_sb[:]), rb[t][:])
+
+        def put_ratio(t):
+            nc.vector.tensor_tensor(y[t][:].indirect(n1_sb[:]), pa[t][:], inv[t][:], ALU.mult)
+            nc.sync.dma_start(out=out_rows[t], in_=y[t][:])
+
         for t in range(PACK):
             u = t + 1
-            nc.vector.tensor_copy(y[t][:].indirect(n2_sb[:]), rb[t][:])
+            if t < 2:
+                put_max(t)
             if u < PACK:
                 nc.scalar.copy(out=h[u][:], in_=acc[u + 1][:])
             nc.scalar.activation(size[t][:], pb[t][:], ACT.Abs)
@@ -121,17 +134,24 @@ def tile_picked_othratio_none_po_kernel(tc, x_words, x_scales, w1, w2, offs, hz,
             nc.scalar.activation(inv[t][:], root[t][:], ACT.Square)
             if u < PACK:
                 nc.vector.tensor_tensor(rb[u][:], pa[u][:], pb[u][:], ALU.max)
-            nc.vector.tensor_tensor(y[t][:].indirect(n1_sb[:]), pa[t][:], inv[t][:], ALU.mult)
-            nc.sync.dma_start(out=out_rows[t], in_=y[t][:])
+            if t < 2:
+                put_ratio(t)
+        for t in range(2, PACK):
+            put_max(t)
+        for t in range(2, PACK):
+            put_ratio(t)
+        rounded = keep.tile([P, PACK, S], BF16, name="rounded", tag="late", align_bytes=64)
         for t in range(PACK - 1):
             nc.scalar.copy(out=rounded[:, t, :], in_=y[t][:])
-        nc.vector.tensor_copy(out=rounded[:, PACK - 1, :], in_=y[PACK - 1][:])
+        shares = ((nc.vector.tensor_copy, slice(0, 256)), (nc.vector.tensor_copy, slice(256, 336)), (nc.scalar.copy, slice(336, S)))
+        for copy, cols in shares:
+            copy(out=rounded[:, PACK - 1, cols], in_=y[PACK - 1][:, cols])
 
         woven = keep.tile([P, S, PACK], BF16, name="woven", align_bytes=64)
         y_codes = keep.tile([P, S], U32, name="y_codes", align_bytes=64)
         y_plane = keep.tile([P, S], U8, name="y_plane", align_bytes=64)
         out_words = out_1[0].rearrange("p c r -> p (c r)").bitcast(I32)
-        for copy, cols in ((nc.vector.tensor_copy, slice(0, 256)), (nc.vector.tensor_copy, slice(256, 320)), (nc.scalar.copy, slice(320, S))):
+        for copy, cols in shares:
             copy(out=woven[:, cols, :].rearrange("p (c i) t -> p c t i", i=4),
                  in_=rounded[:, :, cols].rearrange("p t (c i) -> p c t i", i=4))
         for c in range(2):

from contextlib import ExitStack

import concourse.mybir as mybir

F32 = mybir.dt.float32
BF16 = mybir.dt.bfloat16
I32 = mybir.dt.int32
U32 = mybir.dt.uint32
U16 = mybir.dt.uint16
U8 = mybir.dt.uint8
FP8X4 = mybir.dt.float8_e4m3fn_x4
ACT = mybir.ActivationFunctionType
ALU = mybir.AluOpType

P = 128
PACK = 4
K, T, S, N, W = 512, 2048, 512, 512, 256
HALF = N // 2
FLOPS = 2 * 2 * K * N * S


def tile_picked_othratio_none_po_kernel(tc, x_words, x_scales, w1, w2, offs, hz, n1, n2, out_0, out_1, out_2):
    nc = tc.nc
    with ExitStack() as ctx:
        keep = ctx.enter_context(tc.tile_pool(name="keep", bufs=1))
        psum = ctx.enter_context(tc.psum_pool(name="psum", bufs=1))

        offs_sb = keep.tile([P, S // 16], U16, name="offs_sb")
        hz_sb = keep.tile([P, S // 16], U16, name="hz_sb")
        n1_sb = keep.tile([P, W // 16], U16, name="n1_sb")
        n2_sb = keep.tile([P, W // 16], U16, name="n2_sb")
        table_words = keep.tile([P, T], U32, name="table_words", align_bytes=64)
        table_scales = keep.tile([P, T], U8, name="table_scales", align_bytes=64)
        picked_scales = keep.tile([P, 2 * S], U8, name="picked_scales", align_bytes=64)
        x_planes = keep.tile([P, 2 * S], U8, name="x_planes", align_bytes=64)
        half = keep.tile([P, 1], F32, name="half")

        nc.sync.dma_start(out=table_scales[:].bitcast(I32),
                          in_=x_scales[0].bitcast(I32).unsqueeze(1).to_broadcast([16, 8, T // 4]))
        nc.sync.dma_start(hz_sb[:], hz)
        nc.sync.dma_start(offs_sb[:], offs)
        nc.sync.dma_start(out=table_words[:].bitcast(I32), in_=x_words[0].rearrange("p c r -> p (c r)").bitcast(I32))
        nc.sync.dma_start(n2_sb[:], n2)
        nc.sync.dma_start(n1_sb[:], n1)
        raw1 = keep.tile([P, PACK, N], F32, name="raw1", align_bytes=64)
        nc.sync.dma_start(out=raw1[:], in_=w1.rearrange("(p j) c -> p j c", j=PACK))
        raw = {(0, c): raw1[:, :, c * HALF:(c + 1) * HALF] for c in range(2)}
        for c in range(2):
            raw2 = keep.tile([P, PACK, HALF], F32, name=f"raw2{c}", align_bytes=64)
            nc.sync.dma_start(out=raw2[:], in_=w2[:, c * HALF:(c + 1) * HALF].rearrange("(p j) c -> p j c", j=PACK))
            raw[1, c] = raw2[:]
        nc.gpsimd.memset(half[:], 0.5)
        nc.gpsimd.memset(x_planes[:].bitcast(I32), 0)
        warm = keep.tile([P, 1], F32, name="warm")
        nc.scalar.activation(warm[:], half[:], ACT.Abs_reciprocal_sqrt)

        nc.vector.tensor_copy(picked_scales[:, S:], table_scales[:].indirect(hz_sb[:]))
        nc.vector.tensor_copy(picked_scales[:, :S], table_scales[:].indirect(offs_sb[:]))
        for j in range(PACK):
            nc.scalar.dma_start(out=x_planes[j:P:32, :].bitcast(I32), in_=picked_scales[8 * j:P:32, :].bitcast(I32))
        picked_words = []
        for i, lst in enumerate((offs_sb, hz_sb)):
            words = keep.tile([P, S], U32, name=f"picked_words{i}", align_bytes=64)
            nc.vector.tensor_copy(words[:], table_words[:].indirect(lst[:]))
            picked_words.append(words)

        dealt = keep.tile([P, PACK, 2, P, PACK], BF16, name="dealt", align_bytes=64)
        w_codes = keep.tile([P, 2 * N], U32, name="w_codes", align_bytes=64)
        w_planes = keep.tile([P, 2 * N], U8, name="w_planes", align_bytes=64)

        def deal(copy, i, c, m0, m1):
            base = c * (HALF // PACK)
            copy(out=dealt[:, :, i, base + m0:base + m1, :].rearrange("p t m j -> p m j t"),
                 in_=raw[i, c][:, :, PACK * m0:PACK * m1].rearrange("p j (m t) -> p m j t", t=PACK))

        def quantize_weights(s0, s1):
            nc.vector.quantize_mx(out=w_codes[:, s0 * P:s1 * P].bitcast(FP8X4), scales=w_planes[:, s0 * P:s1 * P],
                                  in_=dealt[:].rearrange("p t i m j -> p (t i m j)")[:, s0 * N:s1 * N])

        deal(nc.scalar.copy, 0, 0, 0, 40)
        deal(nc.vector.tensor_copy, 0, 0, 40, 64)
        deal(nc.vector.tensor_copy, 0, 1, 0, 64)
        quantize_weights(0, 1)
        for c in range(2):
            deal(nc.vector.tensor_copy, 1, c, 0, 44)
            deal(nc.scalar.copy, 1, c, 44, 64)
        quantize_weights(1, 2)
        for t in range(1, PACK):
            quantize_weights(2 * t, 2 * t + 2)

        banks = [(0, slice(0, S // 2)), (0, slice(S // 2, S))] + [(t, slice(0, S)) for t in range(1, PACK)]
        acc = [psum.tile([P, cols.stop - cols.start], F32, name=f"acc{b}") for b, (t, cols) in enumerate(banks)]
        for b, (t, cols) in enumerate(banks):
            for i in range(2):
                rows = slice((2 * t + i) * P, (2 * t + i + 1) * P)
                nc.tensor.matmul_mx(out=acc[b][:], lhsT=w_codes[:, rows].bitcast(FP8X4), lhsT_scale=w_planes[:, rows],
                                    rhs=picked_words[i][:, cols].bitcast(FP8X4),
                                    rhs_scale=x_planes[:, i * S + cols.start:i * S + cols.stop],
                                    start=(i == 0), stop=(i == 1))

        def tiles(name, width):
            return [keep.tile([P, width], F32, name=f"{name}{t}", align_bytes=64) for t in range(PACK)]

        h = [keep.tile([P, S], F32, name="h", tag="row", align_bytes=64)] * PACK
        y = [keep.tile([P, S], F32, name=f"y{t}", tag=("row" if t == 2 else f"y{t}"), align_bytes=64) for t in range(PACK)]
        pa, pb, rb, size, inv = (tiles(name, W) for name in ("pa", "pb", "rb", "size", "inv"))
        root = [keep.tile([P, W], F32, name=f"root{t}", tag=("late" if t == PACK - 1 else f"root{t}"), align_bytes=64) for t in range(PACK)]
        out_rows = out_0.rearrange("(p t) c -> t p c", t=PACK)

        nc.vector.tensor_copy(out=h[0][:, :S // 2], in_=acc[0][:])
        nc.scalar.copy(out=h[0][:, S // 2:], in_=acc[1][:])
        nc.scalar.activation(pb[0][:], h[0][:].indirect(n2_sb[:]), ACT.Copy)
        nc.vector.tensor_copy(pa[0][:], h[0][:].indirect(n1_sb[:]))
        nc.vector.tensor_tensor(rb[0][:], pa[0][:], pb[0][:], ALU.max)
        def put_max(t):
            nc.vector.tensor_copy(y[t][:].indirect(n2_sb[:]), rb[t][:])

        def put_ratio(t):
            nc.vector.tensor_tensor(y[t][:].indirect(n1_sb[:]), pa[t][:], inv[t][:], ALU.mult)
            nc.sync.dma_start(out=out_rows[t], in_=y[t][:])

        for t in range(PACK):
            u = t + 1
            if t < 2:
                put_max(t)
            if u < PACK:
                nc.scalar.copy(out=h[u][:], in_=acc[u + 1][:])
            nc.scalar.activation(size[t][:], pb[t][:], ACT.Abs)
            if u < PACK:
                nc.scalar.activation(pb[u][:], h[u][:].indirect(n2_sb[:]), ACT.Copy)
            nc.scalar.activation(root[t][:], size[t][:], ACT.Abs_reciprocal_sqrt, bias=half[:])
            if u < PACK:
                nc.scalar.activation(pa[u][:], h[u][:].indirect(n1_sb[:]), ACT.Copy)
            nc.scalar.activation(inv[t][:], root[t][:], ACT.Square)
            if u < PACK:
                nc.vector.tensor_tensor(rb[u][:], pa[u][:], pb[u][:], ALU.max)
            if t < 2:
                put_ratio(t)
        for t in range(2, PACK):
            put_max(t)
        for t in range(2, PACK):
            put_ratio(t)
        rounded = keep.tile([P, PACK, S], BF16, name="rounded", tag="late", align_bytes=64)
        for t in range(PACK - 1):
            nc.scalar.copy(out=rounded[:, t, :], in_=y[t][:])
        shares = ((nc.vector.tensor_copy, slice(0, 256)), (nc.vector.tensor_copy, slice(256, 336)), (nc.scalar.copy, slice(336, S)))
        for copy, cols in shares:
            copy(out=rounded[:, PACK - 1, cols], in_=y[PACK - 1][:, cols])

        woven = keep.tile([P, S, PACK], BF16, name="woven", align_bytes=64)
        y_codes = keep.tile([P, S], U32, name="y_codes", align_bytes=64)
        y_plane = keep.tile([P, S], U8, name="y_plane", align_bytes=64)
        out_words = out_1[0].rearrange("p c r -> p (c r)").bitcast(I32)
        for copy, cols in shares:
            copy(out=woven[:, cols, :].rearrange("p (c i) t -> p c t i", i=4),
                 in_=rounded[:, :, cols].rearrange("p t (c i) -> p c t i", i=4))
        for c in range(2):
            cols = slice(c * S // 2, (c + 1) * S // 2)
            nc.vector.quantize_mx(out=y_codes[:, cols].bitcast(FP8X4), scales=y_plane[:, cols],
                                  in_=woven[:, cols, :].rearrange("p c t -> p (c t)"))
            nc.sync.dma_start(out=out_words[:, cols], in_=y_codes[:, cols].bitcast(I32))
        for q in range(4):
            queue = nc.sync if q % 2 == 0 else nc.scalar
            queue.dma_start(out=out_2[0, 4 * q:4 * q + 4, :].bitcast(I32), in_=y_plane[32 * q:32 * q + 4, :].bitcast(I32))
